import numpy as np
import ml_dtypes


def mxq(x, axis, fmt="e4m3"):
    dtype, down = {"e4m3": (ml_dtypes.float8_e4m3fn, 7), "e5m2": (ml_dtypes.float8_e5m2, 14)}[fmt]
    v = np.moveaxis(np.asarray(x, np.float32).astype(ml_dtypes.bfloat16).astype(np.float64), axis, -1)
    blocks = v.reshape(v.shape[:-1] + (-1, 32))
    amax = np.abs(blocks).max(-1, keepdims=True)
    byte = np.maximum(np.where(amax > 0, np.frexp(amax)[1] - 1 + 127, 0) - down, 1)
    scale = np.exp2(byte - 127.0)
    codes = (blocks / scale).astype(np.float32).astype(dtype).astype(np.float64)
    return np.moveaxis((codes * scale).reshape(v.shape), -1, axis)


WIDE = False


def mx_kscale(k):
    if not WIDE:
        return np.ones(k)
    levels = np.array([30, -30])
    if k % 512:
        return np.exp2(np.random.permutation(np.resize(levels, k // 32))).repeat(32)
    a = np.empty((k // 512, 16))
    for p in range(k // 512):
        a[p, :8] = np.random.permutation(np.resize(levels, 8))
        for g in range(8):
            far = levels[np.abs(levels - a[p, g]) >= 10]
            a[p, g + 8] = far[np.random.randint(len(far))]
    return np.exp2(a.ravel()).repeat(32)


def f64(x):
    return np.asarray(x).astype(np.float64)


def striped(idx):
    return np.tile(np.asarray(idx).reshape(-1, 16).T, (8, 1)).astype(np.uint16)


def unstriped(offs):
    return offs[:16].T.reshape(-1).astype(np.int64)


E2M1 = np.array([0.0, 0.5, 1.0, 1.5, 2.0, 3.0, 4.0, 6.0, -0.0, -0.5, -1.0, -1.5, -2.0, -3.0, -4.0, -6.0])


def pack_weight(w, fmt):
    k, n = w.shape
    w = f64(np.asarray(w, np.float32).astype(ml_dtypes.bfloat16)).reshape(k // 32, 32, n)
    amax = np.abs(w).max(1)
    if fmt in ("e4m3", "e5m2"):
        byte = np.frexp(amax)[1] - 1 + 127 - (7 if fmt == "e4m3" else 14)
    else:
        mant, ex = np.frexp(amax / 6.0)
        byte = np.where(mant > 0.5, ex, ex - 1) + 127
    byte = np.clip(np.where(amax > 0, byte, 1), 1, 254)
    scaled = (w * np.exp2(127.0 - byte)[:, None, :]).reshape(k, n).astype(np.float32)
    by_word = np.ascontiguousarray(scaled.reshape(k // 512, 128, 4, n).transpose(0, 1, 3, 2))
    if fmt in ("e4m3", "e5m2"):
        words = by_word.astype(ml_dtypes.float8_e4m3fn if fmt == "e4m3" else ml_dtypes.float8_e5m2).view(np.uint8)
    else:
        c = by_word.astype(ml_dtypes.float4_e2m1fn).view(np.uint8) & 0xF
        words = (c[..., 0::2] | (c[..., 1::2] << 4)).reshape(k // 512, 128, 2 * n)
    return np.ascontiguousarray(words), np.ascontiguousarray(byte.astype(np.uint8).reshape(k // 512, 16, n))


def unpack_weight(words, scales, fmt):
    g, _, n = scales.shape
    words = np.ascontiguousarray(words).reshape(g, 128, n, -1)
    if fmt in ("e4m3", "e5m2"):
        vals = words.view(ml_dtypes.float8_e4m3fn if fmt == "e4m3" else ml_dtypes.float8_e5m2).astype(np.float64)
    else:
        nib = np.empty((g, 128, n, 4), np.uint8)
        nib[..., 0::2] = words & 0xF
        nib[..., 1::2] = words >> 4
        vals = E2M1[nib]
    vals = vals * np.repeat(np.exp2(scales.astype(np.float64) - 127.0), 8, axis=1)[..., None]
    return vals.transpose(0, 1, 3, 2).reshape(g * 512, n)


K, T, J, R, C, O, N, L, E = 512, 2048, 256, 512, 512, 256, 256, 512, 1024


def setup_inputs():
    n = np.random.standard_normal
    idx = np.random.permutation(T)[:J]
    idx2 = np.random.permutation(T)[:J]
    idx3 = np.random.permutation(C)[:J]
    idx4 = np.random.permutation(C)[:J]
    idx5 = np.random.permutation(C)[:O]
    idx6 = np.random.permutation(C)[:O]
    idx7 = np.random.permutation(E)[:O]
    fk = mx_kscale(K)
    fr = mx_kscale(R)
    fl = mx_kscale(L)
    xtp = pack_weight(n((K, T)) / fk[:, None], "e4m3")
    wp = pack_weight(n((K, R)) * 1 / np.sqrt(K) * fk[:, None] * fr, "e2m1")
    w2p = pack_weight(n((K, R)) * 1 / np.sqrt(K) * fk[:, None] * fr, "e5m2")
    wbp = pack_weight(n((R, N)) * 1 / np.sqrt(R) / fr[:, None], "e5m2")
    sxp = pack_weight(n((L, O)) / fl[:, None], "e2m1")
    wsp = pack_weight(n((L, N)) * 1 / np.sqrt(L) * fl[:, None], "e5m2")
    return {
        "xt_words": xtp[0],
        "xt_scales": xtp[1],
        "w_words": wp[0],
        "w_scales": wp[1],
        "w2_words": w2p[0],
        "w2_scales": w2p[1],
        "wb_words": wbp[0],
        "wb_scales": wbp[1],
        "sx_words": sxp[0],
        "sx_scales": sxp[1],
        "ws_words": wsp[0],
        "ws_scales": wsp[1],
        "tz": (n((N, E))).astype(np.float32),
        "offs": striped(idx),
        "offs2": striped(idx2),
        "offs3": striped(idx3),
        "offs4": striped(idx4),
        "offs5": striped(idx5),
        "offs6": striped(idx6),
        "offs7": striped(idx7),
    }


def reference(xt_words, xt_scales, w_words, w_scales, w2_words, w2_scales, wb_words, wb_scales, sx_words, sx_scales, ws_words, ws_scales, tz, offs, offs2, offs3, offs4, offs5, offs6, offs7):
    idx = unstriped(offs)
    idx2 = unstriped(offs2)
    idx3 = unstriped(offs3)
    idx4 = unstriped(offs4)
    idx5 = unstriped(offs5)
    idx6 = unstriped(offs6)
    idx7 = unstriped(offs7)
    xtu = unpack_weight(xt_words, xt_scales, "e4m3")
    wu = unpack_weight(w_words, w_scales, "e2m1")
    w2u = unpack_weight(w2_words, w2_scales, "e5m2")
    wbu = unpack_weight(wb_words, wb_scales, "e5m2")
    sxu = unpack_weight(sx_words, sx_scales, "e2m1")
    wsu = unpack_weight(ws_words, ws_scales, "e5m2")
    xtidxg = xtu[:, idx]
    a = wu.T @ xtidxg
    xtidx2g = xtu[:, idx2]
    b = w2u.T @ xtidx2g
    pw = np.zeros((R, C))
    pw[:, idx3] = a
    pv = np.zeros((R, C))
    pv[:, idx4] = b
    hid = np.maximum(pw[:, idx5], pv[:, idx6])
    hidq = mxq(hid, 0, "e4m3")
    p = wbu.T @ hidq + wsu.T @ sxu
    y = p + f64(tz)[:, idx7]
    return y

@@ -1,0 +1,167 @@
+from contextlib import ExitStack
+
+import concourse.mybir as mybir
+
+K, T, J, R, C, O, N, L, E = 512, 2048, 256, 512, 512, 256, 256, 512, 1024
+FLOPS = 2 * (2 * K * R * J + R * N * O + L * N * O)
+
+F32 = mybir.dt.float32
+BF16 = mybir.dt.bfloat16
+I32 = mybir.dt.int32
+U32 = mybir.dt.uint32
+U16 = mybir.dt.uint16
+U8 = mybir.dt.uint8
+E4M3 = mybir.dt.float8_e4m3fn_x4
+E5M2 = mybir.dt.float8_e5m2_x4
+E2M1 = mybir.dt.float4_e2m1fn_x4
+COPY = mybir.ActivationFunctionType.Copy
+ALU = mybir.AluOpType
+
+P = 128
+PACK = 4
+
+
+def tile_list_ahead_twoboards_skip_tabled_kernel(
+    tc, xt_words, xt_scales, w_words, w_scales, w2_words, w2_scales, wb_words, wb_scales,
+    sx_words, sx_scales, ws_words, ws_scales, tz,
+    offs, offs2, offs3, offs4, offs5, offs6, offs7, out,
+):
+    nc = tc.nc
+    with ExitStack() as ctx:
+        sb = ctx.enter_context(tc.tile_pool(name="sb", bufs=1))
+        psum = ctx.enter_context(tc.psum_pool(name="psum", bufs=1))
+
+        def sbuf(name, shape, dtype):
+            return sb.tile(shape, dtype, name=name, align_bytes=64)
+
+        def load_list(name, src):
+            tile = sbuf(name, [P, J // 16], U16)
+            nc.sync.dma_start(tile[:], src)
+            return tile
+
+        def load_words(name, src):
+            rows = src[0] if src.ndim == 3 else src[0].rearrange("p n t -> p (n t)")
+            tile = sbuf(name, [P, rows.shape[1]], U8)
+            nc.sync.dma_start(tile[:].bitcast(I32), rows.bitcast(I32))
+            return tile
+
+        def load_scales(plane, src):
+            for q in range(4):
+                nc.sync.dma_start(plane[32 * q : 32 * q + 4, :].bitcast(I32), src[0, 4 * q : 4 * q + 4, :].bitcast(I32))
+
+        def move(engine, dst, src):
+            if engine == "vector":
+                nc.vector.tensor_copy(dst, src)
+            else:
+                nc.scalar.activation(dst, src, COPY)
+
+        def dealt(ap):
+            return ap.rearrange("p (m t) -> p t m", t=PACK)
+
+        def quarters(ap):
+            return ap.rearrange("p (t m) -> p t m", t=PACK)
+
+        xt_plane = sbuf("xt_plane", [P, T], U8)
+        nc.vector.memset(xt_plane[:].bitcast(I32), 0)
+        planes = sbuf("planes", [P, 2 * R + 2 * N + O], U8)
+        nc.vector.memset(planes[:].bitcast(I32), 0)
+        w_plane, w2_plane = planes[:, 0:R], planes[:, R : 2 * R]
+        wb_plane = planes[:, 2 * R : 2 * R + N]
+        ws_plane = planes[:, 2 * R + N : 2 * R + 2 * N]
+        sx_plane = planes[:, 2 * R + 2 * N : 2 * R + 2 * N + O]
+        boards = [[sbuf("board%d_%d" % (s, t), [P, C], F32) for t in range(PACK)] for s in range(2)]
+        for s in range(2):
+            for t in range(PACK):
+                nc.vector.memset(boards[s][t][:], 0.0)
+
+        list1 = load_list("list1", offs)
+        w_raw = load_words("w_raw", w_words)
+        load_scales(xt_plane, xt_scales)
+        xt_raw = load_words("xt_raw", xt_words)
+        list2 = load_list("list2", offs2)
+        load_scales(w_plane, w_scales)
+        list3 = load_list("list3", offs3)
+        w2_raw = load_words("w2_raw", w2_words)
+        list5 = load_list("list5", offs5)
+        load_scales(w2_plane, w2_scales)
+        list4 = load_list("list4", offs4)
+        list6 = load_list("list6", offs6)
+        list7 = load_list("list7", offs7)
+        tz_rows = []
+        for h in range(N // P):
+            rows = sbuf("tz%d" % h, [P, E], F32)
+            nc.sync.dma_start(rows[:], tz[h * P : (h + 1) * P, :])
+            tz_rows.append(rows)
+        ws_raw = load_words("ws_raw", ws_words)
+        sx_raw = load_words("sx_raw", sx_words)
+        wb_raw = load_words("wb_raw", wb_words)
+        load_scales(ws_plane, ws_scales)
+        load_scales(sx_plane, sx_scales)
+        load_scales(wb_plane, wb_scales)
+
+        w_codes = sbuf("w_codes", [P, 2 * R], U8)
+        nc.scalar.copy(quarters(w_codes[:].bitcast(U16)), dealt(w_raw[:].bitcast(U16)))
+        x_scale = [sbuf("x_scale%d" % s, [P, J], U8) for s in range(2)]
+        x_codes = [sbuf("x_codes%d" % s, [P, J], U32) for s in range(2)]
+        nc.vector.tensor_copy(x_scale[0][:], xt_plane[:].indirect(list1[:]))
+        nc.vector.tensor_copy(x_scale[1][:], xt_plane[:].indirect(list2[:]))
+        w_scale = sbuf("w_scale", [P, R], U8)
+        nc.vector.tensor_copy(quarters(w_scale[:]), dealt(w_plane))
+        nc.vector.tensor_copy(x_codes[0][:], xt_raw[:].bitcast(U32).indirect(list1[:]))
+        nc.vector.tensor_copy(x_codes[1][:], xt_raw[:].bitcast(U32).indirect(list2[:]))
+        w2_codes = sbuf("w2_codes", [P, R], U32)
+        nc.gpsimd.tensor_copy(quarters(w2_codes[:]), dealt(w2_raw[:].bitcast(U32)))
+        w2_scale = sbuf("w2_scale", [P, R], U8)
+        nc.gpsimd.tensor_copy(quarters(w2_scale[:]), dealt(w2_plane))
+
+        put_lists, take_lists = (list3, list4), (list5, list6)
+        taken = [sbuf("taken%d" % s, [P, PACK, O], F32) for s in range(2)]
+        for s in range(2):
+            for t in range(PACK):
+                cols = slice(t * P, (t + 1) * P)
+                if s == 0:
+                    lhs = w_codes[:, 2 * t * P : 2 * (t + 1) * P].bitcast(E2M1)
+                    lhs_scale = w_scale[:, cols]
+                else:
+                    lhs = w2_codes[:, cols].bitcast(E5M2)
+                    lhs_scale = w2_scale[:, cols]
+                bank = psum.tile([P, J], F32, name="bank", tag="bank%d" % (PACK * s + t))
+                nc.tensor.matmul_mx(
+                    out=bank[:], lhsT=lhs, lhsT_scale=lhs_scale,
+                    rhs=x_codes[s][:].bitcast(E4M3), rhs_scale=x_scale[s][:], start=True, stop=True,
+                )
+                engine = "scalar" if t % 2 == 0 else "vector"
+                sums = sbuf("sums%d_%d" % (s, t), [P, J], F32)
+                move(engine, sums[:], bank[:])
+                move(engine, boards[s][t][:].indirect(put_lists[s][:]), sums[:])
+                move(engine, taken[s][:, t, :], boards[s][t][:].indirect(take_lists[s][:]))
+
+        tz_taken = sbuf("tz_taken", [P, N // P, O], F32)
+        for h in range(N // P):
+            move("scalar", tz_taken[:, h, :], tz_rows[h][:].indirect(list7[:]))
+
+        hid = sbuf("hid", [P, O * PACK], BF16)
+        nc.vector.tensor_tensor(
+            hid[:].rearrange("p (c i t) -> p c t i", i=4, t=PACK),
+            taken[0][:].rearrange("p t (c i) -> p c t i", i=4),
+            taken[1][:].rearrange("p t (c i) -> p c t i", i=4),
+            ALU.max,
+        )
+        hid_codes = sbuf("hid_codes", [P, O], U32)
+        hid_scale = sbuf("hid_scale", [P, O], U8)
+        nc.vector.quantize_mx(out=hid_codes[:].bitcast(E4M3), scales=hid_scale[:], in_=hid[:])
+
+        for h in range(N // P):
+            cols = slice(h * P, (h + 1) * P)
+            bank = psum.tile([P, O], F32, name="bank", tag="bank%d" % h)
+            nc.tensor.matmul_mx(
+                out=bank[:], lhsT=ws_raw[:].bitcast(U32)[:, cols].bitcast(E5M2), lhsT_scale=ws_plane[:, cols],
+                rhs=sx_raw[:].bitcast(E2M1), rhs_scale=sx_plane, start=True, stop=False,
+            )
+            nc.tensor.matmul_mx(
+                out=bank[:], lhsT=wb_raw[:].bitcast(U32)[:, cols].bitcast(E5M2), lhsT_scale=wb_plane[:, cols],
+                rhs=hid_codes[:].bitcast(E4M3), rhs_scale=hid_scale[:], start=False, stop=True,
+            )
+            result = sbuf("result%d" % h, [P, O], F32)
+            nc.vector.tensor_tensor(result[:], bank[:], tz_taken[:, h, :], ALU.add)
+            nc.sync.dma_start(out[cols, :], result[:])

@@ -45,9 +45,9 @@ def tile_list_ahead_twoboards_skip_tabled_kernel(
             nc.sync.dma_start(tile[:].bitcast(I32), rows.bitcast(I32))
             return tile
 
-        def load_scales(plane, src):
-            for q in range(4):
-                nc.sync.dma_start(plane[32 * q : 32 * q + 4, :].bitcast(I32), src[0, 4 * q : 4 * q + 4, :].bitcast(I32))
+        def load_scales(plane, src, queue, quadrants=range(4)):
+            for q in quadrants:
+                queue.dma_start(plane[32 * q : 32 * q + 4, :].bitcast(I32), src[0, 4 * q : 4 * q + 4, :].bitcast(I32))
 
         def move(engine, dst, src):
             if engine == "vector":
@@ -63,51 +63,55 @@ def tile_list_ahead_twoboards_skip_tabled_kernel(
 
         xt_plane = sbuf("xt_plane", [P, T], U8)
         nc.vector.memset(xt_plane[:].bitcast(I32), 0)
-        planes = sbuf("planes", [P, 2 * R + 2 * N + O], U8)
+        w_plane = sb.tile([P, R], U8, name="w_plane", tag="shared", align_bytes=64)
+        nc.vector.memset(w_plane[:].bitcast(I32), 0)
+        planes = sbuf("planes", [P, R + 2 * N + O], U8)
         nc.vector.memset(planes[:].bitcast(I32), 0)
-        w_plane, w2_plane = planes[:, 0:R], planes[:, R : 2 * R]
-        wb_plane = planes[:, 2 * R : 2 * R + N]
-        ws_plane = planes[:, 2 * R + N : 2 * R + 2 * N]
-        sx_plane = planes[:, 2 * R + 2 * N : 2 * R + 2 * N + O]
+        w2_plane = planes[:, 0:R]
+        wb_plane = planes[:, R : R + N]
+        ws_plane = planes[:, R + N : R + 2 * N]
+        sx_plane = planes[:, R + 2 * N : R + 2 * N + O]
         boards = [[sbuf("board%d_%d" % (s, t), [P, C], F32) for t in range(PACK)] for s in range(2)]
         for s in range(2):
             for t in range(PACK):
-                nc.vector.memset(boards[s][t][:], 0.0)
+                nc.vector.memset(boards[s][t][:].bitcast(I32), 0)
 
         list1 = load_list("list1", offs)
-        w_raw = load_words("w_raw", w_words)
-        load_scales(xt_plane, xt_scales)
-        xt_raw = load_words("xt_raw", xt_words)
         list2 = load_list("list2", offs2)
-        load_scales(w_plane, w_scales)
+        w_raw = load_words("w_raw", w_words)
+        load_scales(xt_plane, xt_scales, nc.sync, range(1))
+        xt_raw = load_words("xt_raw", xt_words)
+        load_scales(xt_plane, xt_scales, nc.scalar, range(1, 4))
+        load_scales(w_plane, w_scales, nc.scalar)
         list3 = load_list("list3", offs3)
-        w2_raw = load_words("w2_raw", w2_words)
         list5 = load_list("list5", offs5)
-        load_scales(w2_plane, w2_scales)
+        w2_raw = load_words("w2_raw", w2_words)
+        load_scales(w2_plane, w2_scales, nc.sync)
         list4 = load_list("list4", offs4)
         list6 = load_list("list6", offs6)
+        ws_raw = load_words("ws_raw", ws_words)
+        sx_raw = load_words("sx_raw", sx_words)
+        wb_raw = load_words("wb_raw", wb_words)
         list7 = load_list("list7", offs7)
         tz_rows = []
         for h in range(N // P):
             rows = sbuf("tz%d" % h, [P, E], F32)
             nc.sync.dma_start(rows[:], tz[h * P : (h + 1) * P, :])
             tz_rows.append(rows)
-        ws_raw = load_words("ws_raw", ws_words)
-        sx_raw = load_words("sx_raw", sx_words)
-        wb_raw = load_words("wb_raw", wb_words)
-        load_scales(ws_plane, ws_scales)
-        load_scales(sx_plane, sx_scales)
-        load_scales(wb_plane, wb_scales)
+        load_scales(ws_plane, ws_scales, nc.sync)
+        load_scales(sx_plane, sx_scales, nc.sync)
+        load_scales(wb_plane, wb_scales, nc.sync)
 
         w_codes = sbuf("w_codes", [P, 2 * R], U8)
         nc.scalar.copy(quarters(w_codes[:].bitcast(U16)), dealt(w_raw[:].bitcast(U16)))
         x_scale = [sbuf("x_scale%d" % s, [P, J], U8) for s in range(2)]
-        x_codes = [sbuf("x_codes%d" % s, [P, J], U32) for s in range(2)]
+        x_codes = [sbuf("x_codes0", [P, J], U32)]
         nc.vector.tensor_copy(x_scale[0][:], xt_plane[:].indirect(list1[:]))
         nc.vector.tensor_copy(x_scale[1][:], xt_plane[:].indirect(list2[:]))
         w_scale = sbuf("w_scale", [P, R], U8)
-        nc.vector.tensor_copy(quarters(w_scale[:]), dealt(w_plane))
         nc.vector.tensor_copy(x_codes[0][:], xt_raw[:].bitcast(U32).indirect(list1[:]))
+        nc.vector.tensor_copy(quarters(w_scale[:]), dealt(w_plane[:]))
+        x_codes.append(sb.tile([P, J], U32, name="x_codes1", tag="shared", align_bytes=64))
         nc.vector.tensor_copy(x_codes[1][:], xt_raw[:].bitcast(U32).indirect(list2[:]))
         w2_codes = sbuf("w2_codes", [P, R], U32)
         nc.gpsimd.tensor_copy(quarters(w2_codes[:]), dealt(w2_raw[:].bitcast(U32)))
@@ -141,27 +145,39 @@ def tile_list_ahead_twoboards_skip_tabled_kernel(
             move("scalar", tz_taken[:, h, :], tz_rows[h][:].indirect(list7[:]))
 
         hid = sbuf("hid", [P, O * PACK], BF16)
-        nc.vector.tensor_tensor(
-            hid[:].rearrange("p (c i t) -> p c t i", i=4, t=PACK),
-            taken[0][:].rearrange("p t (c i) -> p c t i", i=4),
-            taken[1][:].rearrange("p t (c i) -> p c t i", i=4),
-            ALU.max,
-        )
         hid_codes = sbuf("hid_codes", [P, O], U32)
         hid_scale = sbuf("hid_scale", [P, O], U8)
-        nc.vector.quantize_mx(out=hid_codes[:].bitcast(E4M3), scales=hid_scale[:], in_=hid[:])
+        halves = [slice(u * P, (u + 1) * P) for u in range(O // P)]
+        for reads in halves:
+            nc.vector.tensor_tensor(
+                hid[:, PACK * reads.start : PACK * reads.stop].rearrange("p (c i t) -> p c t i", i=4, t=PACK),
+                taken[0][:, :, reads].rearrange("p t (c i) -> p c t i", i=4),
+                taken[1][:, :, reads].rearrange("p t (c i) -> p c t i", i=4),
+                ALU.max,
+            )
+        for reads in halves:
+            nc.vector.quantize_mx(
+                out=hid_codes[:, reads].bitcast(E4M3), scales=hid_scale[:, reads],
+                in_=hid[:, PACK * reads.start : PACK * reads.stop],
+            )
 
-        for h in range(N // P):
-            cols = slice(h * P, (h + 1) * P)
-            bank = psum.tile([P, O], F32, name="bank", tag="bank%d" % h)
-            nc.tensor.matmul_mx(
-                out=bank[:], lhsT=ws_raw[:].bitcast(U32)[:, cols].bitcast(E5M2), lhsT_scale=ws_plane[:, cols],
-                rhs=sx_raw[:].bitcast(E2M1), rhs_scale=sx_plane, start=True, stop=False,
-            )
-            nc.tensor.matmul_mx(
-                out=bank[:], lhsT=wb_raw[:].bitcast(U32)[:, cols].bitcast(E5M2), lhsT_scale=wb_plane[:, cols],
-                rhs=hid_codes[:].bitcast(E4M3), rhs_scale=hid_scale[:], start=False, stop=True,
-            )
-            result = sbuf("result%d" % h, [P, O], F32)
-            nc.vector.tensor_tensor(result[:], bank[:], tz_taken[:, h, :], ALU.add)
-            nc.sync.dma_start(out[cols, :], result[:])
+        out_rows = out.rearrange("(h p) o -> p h o", p=P)
+        for u, reads in enumerate(halves):
+            bank = psum.tile([P, N // P, P], F32, name="bank", tag="bank%d" % u)
+            for h in range(N // P):
+                cols = slice(h * P, (h + 1) * P)
+                nc.tensor.matmul_mx(
+                    out=bank[:, h, :], lhsT=ws_raw[:].bitcast(U32)[:, cols].bitcast(E5M2), lhsT_scale=ws_plane[:, cols],
+                    rhs=sx_raw[:, 2 * reads.start : 2 * reads.stop].bitcast(E2M1), rhs_scale=sx_plane[:, reads],
+                    start=(h == 0), stop=False,
+                )
+            for h in range(N // P):
+                cols = slice(h * P, (h + 1) * P)
+                nc.tensor.matmul_mx(
+                    out=bank[:, h, :], lhsT=wb_raw[:].bitcast(U32)[:, cols].bitcast(E5M2), lhsT_scale=wb_plane[:, cols],
+                    rhs=hid_codes[:, reads].bitcast(E4M3), rhs_scale=hid_scale[:, reads],
+                    start=False, stop=(h == N // P - 1),
+                )
+            result = sbuf("result%d" % u, [P, N // P, P], F32)
+            nc.vector.tensor_tensor(result[:], bank[:], tz_taken[:, :, reads], ALU.add)
+            nc.sync.dma_start(out_rows[:, :, reads], result[:])

from contextlib import ExitStack

import concourse.mybir as mybir

K, T, J, R, C, O, N, L, E = 512, 2048, 256, 512, 512, 256, 256, 512, 1024
FLOPS = 2 * (2 * K * R * J + R * N * O + L * N * O)

F32 = mybir.dt.float32
BF16 = mybir.dt.bfloat16
I32 = mybir.dt.int32
U32 = mybir.dt.uint32
U16 = mybir.dt.uint16
U8 = mybir.dt.uint8
E4M3 = mybir.dt.float8_e4m3fn_x4
E5M2 = mybir.dt.float8_e5m2_x4
E2M1 = mybir.dt.float4_e2m1fn_x4
COPY = mybir.ActivationFunctionType.Copy
ALU = mybir.AluOpType

P = 128
PACK = 4


def tile_list_ahead_twoboards_skip_tabled_kernel(
    tc, xt_words, xt_scales, w_words, w_scales, w2_words, w2_scales, wb_words, wb_scales,
    sx_words, sx_scales, ws_words, ws_scales, tz,
    offs, offs2, offs3, offs4, offs5, offs6, offs7, out,
):
    nc = tc.nc
    with ExitStack() as ctx:
        sb = ctx.enter_context(tc.tile_pool(name="sb", bufs=1))
        psum = ctx.enter_context(tc.psum_pool(name="psum", bufs=1))

        def sbuf(name, shape, dtype):
            return sb.tile(shape, dtype, name=name, align_bytes=64)

        def load_list(name, src):
            tile = sbuf(name, [P, J // 16], U16)
            nc.sync.dma_start(tile[:], src)
            return tile

        def load_words(name, src):
            rows = src[0] if src.ndim == 3 else src[0].rearrange("p n t -> p (n t)")
            tile = sbuf(name, [P, rows.shape[1]], U8)
            nc.sync.dma_start(tile[:].bitcast(I32), rows.bitcast(I32))
            return tile

        def load_scales(plane, src, queue, quadrants=range(4)):
            for q in quadrants:
                queue.dma_start(plane[32 * q : 32 * q + 4, :].bitcast(I32), src[0, 4 * q : 4 * q + 4, :].bitcast(I32))

        def move(engine, dst, src):
            if engine == "vector":
                nc.vector.tensor_copy(dst, src)
            else:
                nc.scalar.activation(dst, src, COPY)

        def dealt(ap):
            return ap.rearrange("p (m t) -> p t m", t=PACK)

        def quarters(ap):
            return ap.rearrange("p (t m) -> p t m", t=PACK)

        xt_plane = sbuf("xt_plane", [P, T], U8)
        nc.vector.memset(xt_plane[:].bitcast(I32), 0)
        w_plane = sb.tile([P, R], U8, name="w_plane", tag="shared", align_bytes=64)
        nc.vector.memset(w_plane[:].bitcast(I32), 0)
        planes = sbuf("planes", [P, R + 2 * N + O], U8)
        nc.vector.memset(planes[:].bitcast(I32), 0)
        w2_plane = planes[:, 0:R]
        wb_plane = planes[:, R : R + N]
        ws_plane = planes[:, R + N : R + 2 * N]
        sx_plane = planes[:, R + 2 * N : R + 2 * N + O]
        boards = [[sbuf("board%d_%d" % (s, t), [P, C], F32) for t in range(PACK)] for s in range(2)]
        for s in range(2):
            for t in range(PACK):
                nc.vector.memset(boards[s][t][:].bitcast(I32), 0)

        list1 = load_list("list1", offs)
        list2 = load_list("list2", offs2)
        w_raw = load_words("w_raw", w_words)
        load_scales(xt_plane, xt_scales, nc.sync, range(1))
        xt_raw = load_words("xt_raw", xt_words)
        load_scales(xt_plane, xt_scales, nc.scalar, range(1, 4))
        load_scales(w_plane, w_scales, nc.scalar)
        list3 = load_list("list3", offs3)
        list5 = load_list("list5", offs5)
        w2_raw = load_words("w2_raw", w2_words)
        load_scales(w2_plane, w2_scales, nc.sync)
        list4 = load_list("list4", offs4)
        list6 = load_list("list6", offs6)
        ws_raw = load_words("ws_raw", ws_words)
        sx_raw = load_words("sx_raw", sx_words)
        wb_raw = load_words("wb_raw", wb_words)
        list7 = load_list("list7", offs7)
        tz_rows = []
        for h in range(N // P):
            rows = sbuf("tz%d" % h, [P, E], F32)
            nc.sync.dma_start(rows[:], tz[h * P : (h + 1) * P, :])
            tz_rows.append(rows)
        load_scales(ws_plane, ws_scales, nc.sync)
        load_scales(sx_plane, sx_scales, nc.sync)
        load_scales(wb_plane, wb_scales, nc.sync)

        w_codes = sbuf("w_codes", [P, 2 * R], U8)
        nc.scalar.copy(quarters(w_codes[:].bitcast(U16)), dealt(w_raw[:].bitcast(U16)))
        x_scale = [sbuf("x_scale%d" % s, [P, J], U8) for s in range(2)]
        x_codes = [sbuf("x_codes0", [P, J], U32)]
        nc.vector.tensor_copy(x_scale[0][:], xt_plane[:].indirect(list1[:]))
        nc.vector.tensor_copy(x_scale[1][:], xt_plane[:].indirect(list2[:]))
        w_scale = sbuf("w_scale", [P, R], U8)
        nc.vector.tensor_copy(x_codes[0][:], xt_raw[:].bitcast(U32).indirect(list1[:]))
        nc.vector.tensor_copy(quarters(w_scale[:]), dealt(w_plane[:]))
        x_codes.append(sb.tile([P, J], U32, name="x_codes1", tag="shared", align_bytes=64))
        nc.vector.tensor_copy(x_codes[1][:], xt_raw[:].bitcast(U32).indirect(list2[:]))
        w2_codes = sbuf("w2_codes", [P, R], U32)
        nc.gpsimd.tensor_copy(quarters(w2_codes[:]), dealt(w2_raw[:].bitcast(U32)))
        w2_scale = sbuf("w2_scale", [P, R], U8)
        nc.gpsimd.tensor_copy(quarters(w2_scale[:]), dealt(w2_plane))

        put_lists, take_lists = (list3, list4), (list5, list6)
        taken = [sbuf("taken%d" % s, [P, PACK, O], F32) for s in range(2)]
        for s in range(2):
            for t in range(PACK):
                cols = slice(t * P, (t + 1) * P)
                if s == 0:
                    lhs = w_codes[:, 2 * t * P : 2 * (t + 1) * P].bitcast(E2M1)
                    lhs_scale = w_scale[:, cols]
                else:
                    lhs = w2_codes[:, cols].bitcast(E5M2)
                    lhs_scale = w2_scale[:, cols]
                bank = psum.tile([P, J], F32, name="bank", tag="bank%d" % (PACK * s + t))
                nc.tensor.matmul_mx(
                    out=bank[:], lhsT=lhs, lhsT_scale=lhs_scale,
                    rhs=x_codes[s][:].bitcast(E4M3), rhs_scale=x_scale[s][:], start=True, stop=True,
                )
                engine = "scalar" if t % 2 == 0 else "vector"
                sums = sbuf("sums%d_%d" % (s, t), [P, J], F32)
                move(engine, sums[:], bank[:])
                move(engine, boards[s][t][:].indirect(put_lists[s][:]), sums[:])
                move(engine, taken[s][:, t, :], boards[s][t][:].indirect(take_lists[s][:]))

        tz_taken = sbuf("tz_taken", [P, N // P, O], F32)
        for h in range(N // P):
            move("scalar", tz_taken[:, h, :], tz_rows[h][:].indirect(list7[:]))

        hid = sbuf("hid", [P, O * PACK], BF16)
        hid_codes = sbuf("hid_codes", [P, O], U32)
        hid_scale = sbuf("hid_scale", [P, O], U8)
        halves = [slice(u * P, (u + 1) * P) for u in range(O // P)]
        for reads in halves:
            nc.vector.tensor_tensor(
                hid[:, PACK * reads.start : PACK * reads.stop].rearrange("p (c i t) -> p c t i", i=4, t=PACK),
                taken[0][:, :, reads].rearrange("p t (c i) -> p c t i", i=4),
                taken[1][:, :, reads].rearrange("p t (c i) -> p c t i", i=4),
                ALU.max,
            )
        for reads in halves:
            nc.vector.quantize_mx(
                out=hid_codes[:, reads].bitcast(E4M3), scales=hid_scale[:, reads],
                in_=hid[:, PACK * reads.start : PACK * reads.stop],
            )

        out_rows = out.rearrange("(h p) o -> p h o", p=P)
        for u, reads in enumerate(halves):
            bank = psum.tile([P, N // P, P], F32, name="bank", tag="bank%d" % u)
            for h in range(N // P):
                cols = slice(h * P, (h + 1) * P)
                nc.tensor.matmul_mx(
                    out=bank[:, h, :], lhsT=ws_raw[:].bitcast(U32)[:, cols].bitcast(E5M2), lhsT_scale=ws_plane[:, cols],
                    rhs=sx_raw[:, 2 * reads.start : 2 * reads.stop].bitcast(E2M1), rhs_scale=sx_plane[:, reads],
                    start=(h == 0), stop=False,
                )
            for h in range(N // P):
                cols = slice(h * P, (h + 1) * P)
                nc.tensor.matmul_mx(
                    out=bank[:, h, :], lhsT=wb_raw[:].bitcast(U32)[:, cols].bitcast(E5M2), lhsT_scale=wb_plane[:, cols],
                    rhs=hid_codes[:, reads].bitcast(E4M3), rhs_scale=hid_scale[:, reads],
                    start=False, stop=(h == N // P - 1),
                )
            result = sbuf("result%d" % u, [P, N // P, P], F32)
            nc.vector.tensor_tensor(result[:], bank[:], tz_taken[:, :, reads], ALU.add)
            nc.sync.dma_start(out_rows[:, :, reads], result[:])
